import numpy as np, ml_dtypes
CORES = [10,34,74,98]
N = 4
DEG, TK, TIMES = 4, 64, 3
MASK = [[0,1,2,3],[0,1,2,3],[0,1,2,3],[0,1,2,3]]
def setup_inputs(rng):
    return {"x": rng.standard_normal((N, 128, TK), dtype=np.float32).astype(ml_dtypes.bfloat16), "w": (rng.standard_normal((N, 128, DEG * 128), dtype=np.float32) / np.float32(np.sqrt(128 * DEG / 2))).astype(ml_dtypes.bfloat16)}
def setup_inputs_big(rng):
    d = setup_inputs(rng)
    for k in ("x",): d[k] = (d[k].astype(np.float32) * 1048576.0).astype(d[k].dtype)
    return d
def setup_inputs_small(rng):
    d = setup_inputs(rng)
    for k in ("x",): d[k] = (d[k].astype(np.float32) * (1 / 1048576.0)).astype(d[k].dtype)
    return d
def setup_inputs_apart(rng):
    d = setup_inputs(rng)
    f = (10.0 ** rng.permutation(np.linspace(-1.5, 1.5, N))).astype(np.float32).reshape(N, 1, 1)
    for k in ("x",): d[k] = (d[k].astype(np.float32) * f).astype(d[k].dtype)
    return d
def reference(x, w):
    X, W = x.astype(np.float64), w.astype(np.float64)
    h = list(X)
    for _ in range(TIMES):
        h = [np.maximum(sum(W[r][:, 128 * i:128 * i + 128].T @ h[j] for i, j in enumerate(MASK[r])), 0.0) for r in range(N)]
    return {"y": np.stack(h).astype(ml_dtypes.bfloat16)}

@@ -1,0 +1,132 @@
+from concourse.bass import DstId, RemoteDMATransfer
+from concourse.mybir import AluOpType
+
+N, DEG, TK, P, TIMES = 4, 4, 64, 128, 3
+BLK = TK + DEG * P
+BANK = 512
+
+SCRATCH = {"zeros": ("sbuf", [P, TK], "float32"), "yb": ("sbuf", [P, TK], "bfloat16")}
+SEMAPHORES = ["loaded", "sent", "stored", "zero"]
+for _j in range(N):
+    SCRATCH["blk%d" % _j] = ("sbuf", [P, BLK], "bfloat16")
+    SEMAPHORES.append("arr%d" % _j)
+for _t in range(1, TIMES):
+    SCRATCH["h%d" % _t] = ("sbuf", [P, N * TK], "bfloat16")
+    for _j in range(N):
+        SCRATCH["ps%d_%d" % (_t, _j)] = ("psum", [P, BANK], "float32")
+for _t in range(1, TIMES + 1):
+    for _j in range(N):
+        SEMAPHORES += ["mm%d_%d" % (_t, _j), "relu%d_%d" % (_t, _j)]
+
+
+def _needs(mask, r):
+    need = [None] * (TIMES + 1)
+    need[TIMES] = [r]
+    for t in range(TIMES, 0, -1):
+        need[t - 1] = sorted({m for j in need[t] for m in mask[j]})
+    return need
+
+
+def _blocks(mask, r):
+    return sorted({j for lvl in _needs(mask, r) for j in lvl} - {r})
+
+
+def rank_program(g, core, T, topo):
+    r = T.rank_of(core)
+    if r is None:
+        return
+    mask = T.tables["MASK"]
+    need = _needs(mask, r)
+    sem = T.sem
+    own = T["blk%d" % r]
+
+    def tile(j, i):
+        return T["blk%d" % j][:, TK + P * i:TK + P * (i + 1)]
+
+    g.sync.dma_start(own[:, 0:TK], T.x[:]).then_inc(sem.loaded, 16)
+    g.scalar.dma_start(own[:, TK:BLK], T.w[:]).then_inc(sem.loaded, 16)
+    g.vector.memset(T.zeros[:], 0.0).then_inc(sem.zero, 1)
+
+    dests = [d for d in [(r + k) % N for k in range(1, N)] if r in _blocks(mask, d)]
+    engines = 0
+    if dests:
+        em = topo.mask(core, T.cores[dests[0]])
+        ids = []
+        for d in dests:
+            dc = T.cores[d]
+            if not topo.may_write(core, dc):
+                raise ValueError("core %d may not write to core %d" % (core, dc))
+            em &= topo.mask(core, dc)
+            rid, pid, _se = topo.addr(dc)
+            ids.append(DstId(rid=rid, pnc=pid))
+        engines = bin(em).count("1")
+        g.wait_ge(sem.loaded, 32)
+        g.remote_dma_fused(
+            [RemoteDMATransfer(dst_ids=ids, dma_engine_mask=em, remote_sem=sem["arr%d" % r],
+                               srcs=[own[:]], dsts=[own[:] for _d in dests], alu_op=0)],
+            local_sem=sem.sent)
+
+    te, ve = g.tensor, g.vector
+    ve.wait_ge(sem.zero, 1)
+    count = {}
+
+    def psum(t, j):
+        return T["ps%d_%d" % ((t, j) if t < TIMES else (1, need[1][0]))][:, 0:TK]
+
+    def term(t, j, i, rhs, closed):
+        k = count.get((t, j), 0)
+        count[(t, j)] = k + 1
+        te.matmul(psum(t, j), tile(j, i), rhs, start=(k == 0), stop=(k == DEG - 1)).then_inc(sem["mm%d_%d" % (t, j)], 1)
+        if k == DEG - 1:
+            closed.append(j)
+
+    def relu(t, j):
+        out = T["h%d" % t][:, TK * j:TK * (j + 1)] if t < TIMES else T.yb[:]
+        ve.wait_ge(sem["mm%d_%d" % (t, j)], DEG)
+        ve.tensor_tensor(out, psum(t, j), T.zeros[:], AluOpType.max).then_inc(sem["relu%d_%d" % (t, j)], 1)
+
+    here, issued, closed = [], set(), []
+    for s in [r] + sorted(_blocks(mask, r), key=lambda s: (r - s) % N):
+        if s == r:
+            te.wait_ge(sem.loaded, 32)
+        else:
+            n_in = bin(_send_mask(topo, T, mask, s)).count("1")
+            te.wait_ge(sem["arr%d" % s], n_in)
+        here.append(s)
+        for j in here:
+            if j not in need[1]:
+                continue
+            for i in range(DEG):
+                m = mask[j][i]
+                if m in here and (j, i) not in issued:
+                    issued.add((j, i))
+                    term(1, j, i, T["blk%d" % m][:, 0:TK], closed)
+    for j in closed:
+        relu(1, j)
+
+    for t in range(2, TIMES + 1):
+        prev, closed = closed, []
+        for m in prev:
+            te.wait_ge(sem["relu%d_%d" % (t - 1, m)], 1)
+            for j in need[t]:
+                for i in range(DEG):
+                    if mask[j][i] == m:
+                        term(t, j, i, T["h%d" % (t - 1)][:, TK * m:TK * (m + 1)], closed)
+        for j in closed:
+            relu(t, j)
+
+    g.sync.wait_ge(sem["relu%d_%d" % (TIMES, r)], 1)
+    g.sync.dma_start(T.y[:], T.yb[:]).then_inc(sem.stored, 16)
+    g.sync.wait_ge(sem.stored, 16)
+    if engines:
+        g.wait_ge(sem.sent, engines)
+
+
+def _send_mask(topo, T, mask, s):
+    sc = T.cores[s]
+    em = None
+    for d in range(N):
+        if d != s and s in _blocks(mask, d):
+            e = topo.mask(sc, T.cores[d])
+            em = e if em is None else em & e
+    return em

@@ -5,11 +5,12 @@ N, DEG, TK, P, TIMES = 4, 4, 64, 128, 3
 BLK = TK + DEG * P
 BANK = 512
 
-SCRATCH = {"zeros": ("sbuf", [P, TK], "float32"), "yb": ("sbuf", [P, TK], "bfloat16")}
-SEMAPHORES = ["loaded", "sent", "stored", "zero"]
+SCRATCH = {"zeros": ("sbuf", [P, TK], "float32"), "yb": ("sbuf", [P, TK], "bfloat16"),
+           "xd": ("dram", [P, TK], "bfloat16")}
+SEMAPHORES = ["xs", "xl", "wl", "sent", "stored", "zero"]
 for _j in range(N):
     SCRATCH["blk%d" % _j] = ("sbuf", [P, BLK], "bfloat16")
-    SEMAPHORES.append("arr%d" % _j)
+    SEMAPHORES += ["arr%d" % _j, "xe%d" % _j]
 for _t in range(1, TIMES):
     SCRATCH["h%d" % _t] = ("sbuf", [P, N * TK], "bfloat16")
     for _j in range(N):
@@ -31,6 +32,23 @@ def _blocks(mask, r):
     return sorted({j for lvl in _needs(mask, r) for j in lvl} - {r})
 
 
+def _order(mask, s):
+    return [q for q in [(s + k) % N for k in range(1, N)] if s in _blocks(mask, q)]
+
+
+def _plan(mask, s):
+    d = _order(mask, s)
+    return (d[:-1], d[-1]) if len(d) > 1 else (d, None)
+
+
+def _engines(topo, T, mask, s):
+    em = None
+    for d in _order(mask, s):
+        e = topo.mask(T.cores[s], T.cores[d])
+        em = e if em is None else em & e
+    return em
+
+
 def rank_program(g, core, T, topo):
     r = T.rank_of(core)
     if r is None:
@@ -39,94 +57,103 @@ def rank_program(g, core, T, topo):
     need = _needs(mask, r)
     sem = T.sem
     own = T["blk%d" % r]
+    te, ve = g.tensor, g.vector
+    first, last = _plan(mask, r)
 
-    def tile(j, i):
-        return T["blk%d" % j][:, TK + P * i:TK + P * (i + 1)]
+    if last is not None:
+        g.sync.dma_start(T.xd[:], T.x[:]).then_inc(sem.xs, 16)
+    g.scalar.dma_start(own[:, TK:BLK], T.w[:]).then_inc(sem.wl, 16)
+    g.sync.dma_start(own[:, 0:TK], T.x[:]).then_inc(sem.xl, 16)
+    ve.memset(T.zeros[:], 0.0).then_inc(sem.zero, 1)
+    ve.wait_ge(sem.zero, 1)
 
-    g.sync.dma_start(own[:, 0:TK], T.x[:]).then_inc(sem.loaded, 16)
-    g.scalar.dma_start(own[:, TK:BLK], T.w[:]).then_inc(sem.loaded, 16)
-    g.vector.memset(T.zeros[:], 0.0).then_inc(sem.zero, 1)
+    em = _engines(topo, T, mask, r)
+    calls = [0]
 
-    dests = [d for d in [(r + k) % N for k in range(1, N)] if r in _blocks(mask, d)]
-    engines = 0
-    if dests:
-        em = topo.mask(core, T.cores[dests[0]])
+    def send(dests, src, lo, hi, name):
         ids = []
         for d in dests:
             dc = T.cores[d]
             if not topo.may_write(core, dc):
                 raise ValueError("core %d may not write to core %d" % (core, dc))
-            em &= topo.mask(core, dc)
             rid, pid, _se = topo.addr(dc)
             ids.append(DstId(rid=rid, pnc=pid))
-        engines = bin(em).count("1")
-        g.wait_ge(sem.loaded, 32)
         g.remote_dma_fused(
-            [RemoteDMATransfer(dst_ids=ids, dma_engine_mask=em, remote_sem=sem["arr%d" % r],
-                               srcs=[own[:]], dsts=[own[:] for _d in dests], alu_op=0)],
+            [RemoteDMATransfer(dst_ids=ids, dma_engine_mask=em, remote_sem=sem[name % r],
+                               srcs=[src], dsts=[own[:, lo:hi] for _d in dests], alu_op=0)],
             local_sem=sem.sent)
+        calls[0] += 1
 
-    te, ve = g.tensor, g.vector
-    ve.wait_ge(sem.zero, 1)
-    count = {}
+    if last is not None:
+        g.wait_ge(sem.xs, 16)
+        send([last], T.xd[:], 0, TK, "xe%d")
+    g.wait_ge(sem.xl, 16)
+    g.wait_ge(sem.wl, 16)
+    if first:
+        send(first, own[:], 0, BLK, "arr%d")
+    if last is not None:
+        send([last], own[:, TK:BLK], TK, BLK, "arr%d")
+
+    have_x, have_w = [], []
+    closed = {t: [] for t in range(1, TIMES + 1)}
+    count, issued, waited = {}, set(), set()
 
     def psum(t, j):
         return T["ps%d_%d" % ((t, j) if t < TIMES else (1, need[1][0]))][:, 0:TK]
 
-    def term(t, j, i, rhs, closed):
+    def wait_relu(t, m):
+        if (t, m) not in waited:
+            waited.add((t, m))
+            te.wait_ge(sem["relu%d_%d" % (t, m)], 1)
+
+    def term(t, j, i, m):
+        if t == 1:
+            rhs = T["blk%d" % m][:, 0:TK]
+        else:
+            wait_relu(t - 1, m)
+            rhs = T["h%d" % (t - 1)][:, TK * m:TK * (m + 1)]
+        if t == TIMES:
+            wait_relu(1, need[1][0])
         k = count.get((t, j), 0)
         count[(t, j)] = k + 1
-        te.matmul(psum(t, j), tile(j, i), rhs, start=(k == 0), stop=(k == DEG - 1)).then_inc(sem["mm%d_%d" % (t, j)], 1)
+        te.matmul(psum(t, j), T["blk%d" % j][:, TK + P * i:TK + P * (i + 1)], rhs,
+                  start=(k == 0), stop=(k == DEG - 1)).then_inc(sem["mm%d_%d" % (t, j)], 1)
         if k == DEG - 1:
-            closed.append(j)
+            closed[t].append(j)
+            out = T["h%d" % t][:, TK * j:TK * (j + 1)] if t < TIMES else T.yb[:]
+            ve.wait_ge(sem["mm%d_%d" % (t, j)], DEG)
+            ve.tensor_tensor(out, psum(t, j), T.zeros[:], AluOpType.max).then_inc(sem["relu%d_%d" % (t, j)], 1)
 
-    def relu(t, j):
-        out = T["h%d" % t][:, TK * j:TK * (j + 1)] if t < TIMES else T.yb[:]
-        ve.wait_ge(sem["mm%d_%d" % (t, j)], DEG)
-        ve.tensor_tensor(out, psum(t, j), T.zeros[:], AluOpType.max).then_inc(sem["relu%d_%d" % (t, j)], 1)
+    def pump():
+        for t in range(1, TIMES + 1):
+            for m in list(have_x if t == 1 else closed[t - 1]):
+                for j in have_w:
+                    if j in need[t]:
+                        for i in range(DEG):
+                            if mask[j][i] == m and (t, j, i) not in issued:
+                                issued.add((t, j, i))
+                                term(t, j, i, m)
 
-    here, issued, closed = [], set(), []
-    for s in [r] + sorted(_blocks(mask, r), key=lambda s: (r - s) % N):
-        if s == r:
-            te.wait_ge(sem.loaded, 32)
-        else:
-            n_in = bin(_send_mask(topo, T, mask, s)).count("1")
-            te.wait_ge(sem["arr%d" % s], n_in)
-        here.append(s)
-        for j in here:
-            if j not in need[1]:
-                continue
-            for i in range(DEG):
-                m = mask[j][i]
-                if m in here and (j, i) not in issued:
-                    issued.add((j, i))
-                    term(1, j, i, T["blk%d" % m][:, 0:TK], closed)
-    for j in closed:
-        relu(1, j)
-
-    for t in range(2, TIMES + 1):
-        prev, closed = closed, []
-        for m in prev:
-            te.wait_ge(sem["relu%d_%d" % (t - 1, m)], 1)
-            for j in need[t]:
-                for i in range(DEG):
-                    if mask[j][i] == m:
-                        term(t, j, i, T["h%d" % (t - 1)][:, TK * m:TK * (m + 1)], closed)
-        for j in closed:
-            relu(t, j)
+    srcs = sorted(_blocks(mask, r), key=lambda s: _order(mask, s).index(r))
+    te.wait_ge(sem.xl, 16)
+    te.wait_ge(sem.wl, 16)
+    have_x.append(r)
+    have_w.append(r)
+    pump()
+    for s in srcs:
+        if _plan(mask, s)[1] == r:
+            te.wait_ge(sem["xe%d" % s], bin(_engines(topo, T, mask, s)).count("1"))
+            have_x.append(s)
+            pump()
+    for s in srcs:
+        te.wait_ge(sem["arr%d" % s], bin(_engines(topo, T, mask, s)).count("1"))
+        if s not in have_x:
+            have_x.append(s)
+        have_w.append(s)
+        pump()
 
     g.sync.wait_ge(sem["relu%d_%d" % (TIMES, r)], 1)
     g.sync.dma_start(T.y[:], T.yb[:]).then_inc(sem.stored, 16)
     g.sync.wait_ge(sem.stored, 16)
-    if engines:
-        g.wait_ge(sem.sent, engines)
-
-
-def _send_mask(topo, T, mask, s):
-    sc = T.cores[s]
-    em = None
-    for d in range(N):
-        if d != s and s in _blocks(mask, d):
-            e = topo.mask(sc, T.cores[d])
-            em = e if em is None else em & e
-    return em
+    if calls[0]:
+        g.wait_ge(sem.sent, calls[0] * bin(em).count("1"))

from concourse.bass import DstId, RemoteDMATransfer
from concourse.mybir import AluOpType

N, DEG, TK, P, TIMES = 4, 4, 64, 128, 3
BLK = TK + DEG * P
BANK = 512

SCRATCH = {"zeros": ("sbuf", [P, TK], "float32"), "yb": ("sbuf", [P, TK], "bfloat16"),
           "xd": ("dram", [P, TK], "bfloat16")}
SEMAPHORES = ["xs", "xl", "wl", "sent", "stored", "zero"]
for _j in range(N):
    SCRATCH["blk%d" % _j] = ("sbuf", [P, BLK], "bfloat16")
    SEMAPHORES += ["arr%d" % _j, "xe%d" % _j]
for _t in range(1, TIMES):
    SCRATCH["h%d" % _t] = ("sbuf", [P, N * TK], "bfloat16")
    for _j in range(N):
        SCRATCH["ps%d_%d" % (_t, _j)] = ("psum", [P, BANK], "float32")
for _t in range(1, TIMES + 1):
    for _j in range(N):
        SEMAPHORES += ["mm%d_%d" % (_t, _j), "relu%d_%d" % (_t, _j)]


def _needs(mask, r):
    need = [None] * (TIMES + 1)
    need[TIMES] = [r]
    for t in range(TIMES, 0, -1):
        need[t - 1] = sorted({m for j in need[t] for m in mask[j]})
    return need


def _blocks(mask, r):
    return sorted({j for lvl in _needs(mask, r) for j in lvl} - {r})


def _order(mask, s):
    return [q for q in [(s + k) % N for k in range(1, N)] if s in _blocks(mask, q)]


def _plan(mask, s):
    d = _order(mask, s)
    return (d[:-1], d[-1]) if len(d) > 1 else (d, None)


def _engines(topo, T, mask, s):
    em = None
    for d in _order(mask, s):
        e = topo.mask(T.cores[s], T.cores[d])
        em = e if em is None else em & e
    return em


def rank_program(g, core, T, topo):
    r = T.rank_of(core)
    if r is None:
        return
    mask = T.tables["MASK"]
    need = _needs(mask, r)
    sem = T.sem
    own = T["blk%d" % r]
    te, ve = g.tensor, g.vector
    first, last = _plan(mask, r)

    if last is not None:
        g.sync.dma_start(T.xd[:], T.x[:]).then_inc(sem.xs, 16)
    g.scalar.dma_start(own[:, TK:BLK], T.w[:]).then_inc(sem.wl, 16)
    g.sync.dma_start(own[:, 0:TK], T.x[:]).then_inc(sem.xl, 16)
    ve.memset(T.zeros[:], 0.0).then_inc(sem.zero, 1)
    ve.wait_ge(sem.zero, 1)

    em = _engines(topo, T, mask, r)
    calls = [0]

    def send(dests, src, lo, hi, name):
        ids = []
        for d in dests:
            dc = T.cores[d]
            if not topo.may_write(core, dc):
                raise ValueError("core %d may not write to core %d" % (core, dc))
            rid, pid, _se = topo.addr(dc)
            ids.append(DstId(rid=rid, pnc=pid))
        g.remote_dma_fused(
            [RemoteDMATransfer(dst_ids=ids, dma_engine_mask=em, remote_sem=sem[name % r],
                               srcs=[src], dsts=[own[:, lo:hi] for _d in dests], alu_op=0)],
            local_sem=sem.sent)
        calls[0] += 1

    if last is not None:
        g.wait_ge(sem.xs, 16)
        send([last], T.xd[:], 0, TK, "xe%d")
    g.wait_ge(sem.xl, 16)
    g.wait_ge(sem.wl, 16)
    if first:
        send(first, own[:], 0, BLK, "arr%d")
    if last is not None:
        send([last], own[:, TK:BLK], TK, BLK, "arr%d")

    have_x, have_w = [], []
    closed = {t: [] for t in range(1, TIMES + 1)}
    count, issued, waited = {}, set(), set()

    def psum(t, j):
        return T["ps%d_%d" % ((t, j) if t < TIMES else (1, need[1][0]))][:, 0:TK]

    def wait_relu(t, m):
        if (t, m) not in waited:
            waited.add((t, m))
            te.wait_ge(sem["relu%d_%d" % (t, m)], 1)

    def term(t, j, i, m):
        if t == 1:
            rhs = T["blk%d" % m][:, 0:TK]
        else:
            wait_relu(t - 1, m)
            rhs = T["h%d" % (t - 1)][:, TK * m:TK * (m + 1)]
        if t == TIMES:
            wait_relu(1, need[1][0])
        k = count.get((t, j), 0)
        count[(t, j)] = k + 1
        te.matmul(psum(t, j), T["blk%d" % j][:, TK + P * i:TK + P * (i + 1)], rhs,
                  start=(k == 0), stop=(k == DEG - 1)).then_inc(sem["mm%d_%d" % (t, j)], 1)
        if k == DEG - 1:
            closed[t].append(j)
            out = T["h%d" % t][:, TK * j:TK * (j + 1)] if t < TIMES else T.yb[:]
            ve.wait_ge(sem["mm%d_%d" % (t, j)], DEG)
            ve.tensor_tensor(out, psum(t, j), T.zeros[:], AluOpType.max).then_inc(sem["relu%d_%d" % (t, j)], 1)

    def pump():
        for t in range(1, TIMES + 1):
            for m in list(have_x if t == 1 else closed[t - 1]):
                for j in have_w:
                    if j in need[t]:
                        for i in range(DEG):
                            if mask[j][i] == m and (t, j, i) not in issued:
                                issued.add((t, j, i))
                                term(t, j, i, m)

    srcs = sorted(_blocks(mask, r), key=lambda s: _order(mask, s).index(r))
    te.wait_ge(sem.xl, 16)
    te.wait_ge(sem.wl, 16)
    have_x.append(r)
    have_w.append(r)
    pump()
    for s in srcs:
        if _plan(mask, s)[1] == r:
            te.wait_ge(sem["xe%d" % s], bin(_engines(topo, T, mask, s)).count("1"))
            have_x.append(s)
            pump()
    for s in srcs:
        te.wait_ge(sem["arr%d" % s], bin(_engines(topo, T, mask, s)).count("1"))
        if s not in have_x:
            have_x.append(s)
        have_w.append(s)
        pump()

    g.sync.wait_ge(sem["relu%d_%d" % (TIMES, r)], 1)
    g.sync.dma_start(T.y[:], T.yb[:]).then_inc(sem.stored, 16)
    g.sync.wait_ge(sem.stored, 16)
    if calls[0]:
        g.wait_ge(sem.sent, calls[0] * bin(em).count("1"))
